import numpy as np, ml_dtypes
CORES = [4,20,60,84,92,100,116]
N = 7
R, TK = 64, 16
def setup_inputs(rng):
    u = (rng.standard_normal((N, 128, R), dtype=np.float32) / 11).astype(ml_dtypes.bfloat16)
    return {"x": rng.standard_normal((N, 128, TK), dtype=np.float32).astype(ml_dtypes.bfloat16), "u": u, "ut": u.transpose(0, 2, 1).copy(), "vt": rng.standard_normal((N, R, 128), dtype=np.float32).astype(ml_dtypes.bfloat16)}
def setup_inputs_big(rng):
    d = setup_inputs(rng)
    for k in ("x", "u", "ut", "vt"): d[k] = (d[k].astype(np.float32) * 1024.0).astype(d[k].dtype)
    return d
def setup_inputs_small(rng):
    d = setup_inputs(rng)
    for k in ("x", "u", "ut", "vt"): d[k] = (d[k].astype(np.float32) * (1 / 1024.0)).astype(d[k].dtype)
    return d
def setup_inputs_apart(rng):
    d = setup_inputs(rng)
    f = (10.0 ** rng.permutation(np.linspace(-1.5, 1.5, N))).astype(np.float32).reshape(N, 1, 1)
    for k in ("x", "u", "ut", "vt"): d[k] = (d[k].astype(np.float32) * f).astype(d[k].dtype)
    return d
def tie_inputs(x):
    x = dict(x)
    x["ut"] = x["u"].transpose(0, 2, 1).copy()
    return x
def reference(x, u, ut, vt):
    X, U, VT = x.astype(np.float64), u.astype(np.float64), vt.astype(np.float64)
    y = np.stack([sum(VT[j].T @ (U[j].T @ X[r]) for j in range(N)) for r in range(N)])
    return {"y": y.astype(ml_dtypes.bfloat16 if x.dtype != np.float64 else np.float64)}

@@ -1,0 +1,135 @@
+from concourse.bass import DstId, RemoteDMATransfer
+
+N = 7
+NCORES = 128
+PER_RELAY = 2
+K_RANK = 8
+K_RELAY = 8
+
+SCRATCH = {
+    "utb": ("sbuf", [64, 128], "bfloat16"),
+    "vtb": ("sbuf", [64, 128], "bfloat16"),
+    "xb": ("sbuf", [128, 16], "bfloat16"),
+    "ysb": ("sbuf", [128, 16], "bfloat16"),
+    "pw": ("psum", [128, 512], "float32"),
+    "py": ("psum", [128, 512], "float32"),
+}
+for _j in range(N):
+    SCRATCH["w%d" % _j] = ("sbuf", [128, 128], "bfloat16")
+
+SEMAPHORES = ["ld", "ldx", "mm", "wr", "sent", "done", "yr", "st"] + ["arr%d" % _j for _j in range(N)]
+
+
+def _count(mask):
+    return bin(mask).count("1")
+
+
+def _engines(mask, k):
+    out, bit = 0, 1
+    while _count(out) < k and bit <= mask:
+        out |= mask & bit
+        bit <<= 1
+    return out
+
+
+def _common(topo, src, dsts, k):
+    m = topo.mask(src, dsts[0])
+    for d in dsts[1:]:
+        m &= topo.mask(src, d)
+    return _engines(m, k)
+
+
+def _plan(cores, topo):
+    near, far, load = {}, {}, {}
+    for i, s in enumerate(cores):
+        turn = cores[i + 1:] + cores[:i]
+        near[s] = [d for d in turn if topo.may_write(s, d)]
+        far[s] = [d for d in turn if not topo.may_write(s, d)]
+        for d in near[s]:
+            key = (d, topo.die(s))
+            load[key] = load.get(key, 0) + 1
+    relays = {}
+    for s in cores:
+        ports = [c for c in range(NCORES)
+                 if topo.chip(c) == topo.chip(s) and c not in cores and all(topo.may_write(c, d) for d in far[s])]
+        n = -(-len(far[s]) // PER_RELAY)
+        chosen = {}
+        for d in far[s]:
+            cand = [c for c in ports if (len(chosen[c]) < PER_RELAY if c in chosen else len(chosen) < n)]
+            best = min(cand, key=lambda c: (load.get((d, topo.die(c)), 0), c))
+            chosen.setdefault(best, []).append(d)
+            key = (d, topo.die(best))
+            load[key] = load.get(key, 0) + 1
+        relays[s] = sorted(chosen.items(), key=lambda kv: (-len(kv[1]), kv[0]))
+    return near, relays
+
+
+def _send(g, T, topo, j, dsts, mask):
+    ids = []
+    for d in dsts:
+        rid, pid, _se = topo.addr(d)
+        ids.append(DstId(rid=rid, pnc=pid))
+    buf = T["w%d" % j]
+    g.remote_dma_fused(
+        [RemoteDMATransfer(dst_ids=ids, dma_engine_mask=mask, remote_sem=T.sem["arr%d" % j],
+                           srcs=[buf[:]], dsts=[buf[:] for _d in dsts], alu_op=0)],
+        local_sem=T.sem.sent)
+    return _count(mask)
+
+
+def rank_program(g, core, T, topo):
+    cores = list(T.cores)
+    near, relays = _plan(cores, topo)
+    rank = T.rank_of(core)
+
+    if rank is None:
+        for j, s in enumerate(cores):
+            for h, dsts in relays[s]:
+                if h == core:
+                    helpers = [r for r, _d in relays[s]]
+                    g.wait_ge(T.sem["arr%d" % j], _count(_common(topo, s, helpers + near[s], K_RANK)))
+                    left = _send(g, T, topo, j, dsts, _common(topo, core, dsts, K_RELAY))
+                    g.wait_ge(T.sem.sent, left)
+        return
+
+    mine = T["w%d" % rank]
+    g.sync.dma_start(T.utb[:], T.ut[:]).then_inc(T.sem.ld, 16)
+    g.scalar.dma_start(T.vtb[:], T.vt[:]).then_inc(T.sem.ld, 16)
+    g.sync.dma_start(T.xb[:], T.x[:]).then_inc(T.sem.ldx, 16)
+
+    g.tensor.wait_ge(T.sem.ld, 32)
+    g.tensor.matmul(T.pw[:, 0:128], T.utb[:], T.vtb[:], True, True).then_inc(T.sem.mm, 1)
+    g.vector.wait_ge(T.sem.mm, 1)
+    g.vector.tensor_copy(mine[:], T.pw[:, 0:128]).then_inc(T.sem.wr, 1)
+
+    helpers = [h for h, _d in relays[core]]
+    mask = _common(topo, core, helpers + near[core], K_RANK)
+    g.wait_ge(T.sem.wr, 1)
+    left = 0
+    if helpers:
+        left += _send(g, T, topo, rank, helpers, mask)
+    if near[core]:
+        left += _send(g, T, topo, rank, near[core], mask)
+
+    g.tensor.wait_ge(T.sem.wr, 1)
+    g.tensor.wait_ge(T.sem.ldx, 16)
+    g.tensor.matmul(T.py[:, 0:16], mine[:], T.xb[:], True, False)
+    order = []
+    for j, s in enumerate(cores):
+        if core in near[s]:
+            order.append((j, _count(_common(topo, s, [h for h, _d in relays[s]] + near[s], K_RANK))))
+    for j, s in enumerate(cores):
+        for h, dsts in relays[s]:
+            if core in dsts:
+                order.append((j, _count(_common(topo, h, dsts, K_RELAY))))
+    for n, (j, cnt) in enumerate(order):
+        g.tensor.wait_ge(T.sem["arr%d" % j], cnt)
+        mm = g.tensor.matmul(T.py[:, 0:16], T["w%d" % j][:], T.xb[:], False, n == len(order) - 1)
+    mm.then_inc(T.sem.done, 1)
+
+    g.vector.wait_ge(T.sem.done, 1)
+    g.vector.tensor_copy(T.ysb[:], T.py[:, 0:16]).then_inc(T.sem.yr, 1)
+    g.sync.wait_ge(T.sem.yr, 1)
+    g.sync.dma_start(T.y[:], T.ysb[:]).then_inc(T.sem.st, 16)
+    g.sync.wait_ge(T.sem.st, 16)
+    g.wait_ge(T.sem.sent, left)

@@ -2,22 +2,33 @@ from concourse.bass import DstId, RemoteDMATransfer
 
 N = 7
 NCORES = 128
-PER_RELAY = 2
-K_RANK = 8
+K_FEED = 4
+K_NEAR = 8
 K_RELAY = 8
+H = 64
 
 SCRATCH = {
+    "ud": ("dram", [128, 64], "bfloat16"),
+    "vd": ("dram", [128, 64], "bfloat16"),
     "utb": ("sbuf", [64, 128], "bfloat16"),
     "vtb": ("sbuf", [64, 128], "bfloat16"),
     "xb": ("sbuf", [128, 16], "bfloat16"),
     "ysb": ("sbuf", [128, 16], "bfloat16"),
     "pw": ("psum", [128, 512], "float32"),
-    "py": ("psum", [128, 512], "float32"),
+    "py0": ("psum", [128, 512], "float32"),
+    "py1": ("psum", [128, 512], "float32"),
 }
 for _j in range(N):
     SCRATCH["w%d" % _j] = ("sbuf", [128, 128], "bfloat16")
+    SCRATCH["ua%d" % _j] = ("sbuf", [128, 64], "bfloat16")
+    SCRATCH["vb%d" % _j] = ("sbuf", [128, 64], "bfloat16")
+    SCRATCH["tb%d" % _j] = ("sbuf", [128, 16], "bfloat16")
+for _i in range(5):
+    SCRATCH["pt%d" % _i] = ("psum", [128, 512], "float32")
 
-SEMAPHORES = ["ld", "ldx", "mm", "wr", "sent", "done", "yr", "st"] + ["arr%d" % _j for _j in range(N)]
+SEMAPHORES = ["lu", "lv", "ld", "ldx", "mm", "wr", "sent", "done", "yr", "st", "au", "av"]
+for _j in range(N):
+    SEMAPHORES += ["arr%d" % _j, "su%d" % _j, "sv%d" % _j, "tm%d" % _j, "tc%d" % _j]
 
 
 def _count(mask):
@@ -52,27 +63,26 @@ def _plan(cores, topo):
     for s in cores:
         ports = [c for c in range(NCORES)
                  if topo.chip(c) == topo.chip(s) and c not in cores and all(topo.may_write(c, d) for d in far[s])]
-        n = -(-len(far[s]) // PER_RELAY)
         chosen = {}
+        for c in ports:
+            chosen[c] = []
         for d in far[s]:
-            cand = [c for c in ports if (len(chosen[c]) < PER_RELAY if c in chosen else len(chosen) < n)]
-            best = min(cand, key=lambda c: (load.get((d, topo.die(c)), 0), c))
-            chosen.setdefault(best, []).append(d)
+            best = min(ports, key=lambda c: (len(chosen[c]), load.get((d, topo.die(c)), 0), c))
+            chosen[best].append(d)
             key = (d, topo.die(best))
             load[key] = load.get(key, 0) + 1
-        relays[s] = sorted(chosen.items(), key=lambda kv: (-len(kv[1]), kv[0]))
+        relays[s] = sorted([kv for kv in chosen.items() if kv[1]], key=lambda kv: (-len(kv[1]), kv[0]))
     return near, relays
 
 
-def _send(g, T, topo, j, dsts, mask):
+def _send(g, T, topo, src, dst, sem, dsts, mask):
     ids = []
     for d in dsts:
         rid, pid, _se = topo.addr(d)
         ids.append(DstId(rid=rid, pnc=pid))
-    buf = T["w%d" % j]
     g.remote_dma_fused(
-        [RemoteDMATransfer(dst_ids=ids, dma_engine_mask=mask, remote_sem=T.sem["arr%d" % j],
-                           srcs=[buf[:]], dsts=[buf[:] for _d in dsts], alu_op=0)],
+        [RemoteDMATransfer(dst_ids=ids, dma_engine_mask=mask, remote_sem=sem,
+                           srcs=[src[:]], dsts=[dst[:] for _d in dsts], alu_op=0)],
         local_sem=T.sem.sent)
     return _count(mask)
 
@@ -82,20 +92,32 @@ def rank_program(g, core, T, topo):
     near, relays = _plan(cores, topo)
     rank = T.rank_of(core)
 
+    def feed_mask(s):
+        return _common(topo, s, [h for h, _d in relays[s]] + near[s], K_FEED)
+
+    def near_mask(s):
+        return _common(topo, s, [h for h, _d in relays[s]] + near[s], K_NEAR)
+
     if rank is None:
         for j, s in enumerate(cores):
             for h, dsts in relays[s]:
                 if h == core:
-                    helpers = [r for r, _d in relays[s]]
-                    g.wait_ge(T.sem["arr%d" % j], _count(_common(topo, s, helpers + near[s], K_RANK)))
-                    left = _send(g, T, topo, j, dsts, _common(topo, core, dsts, K_RELAY))
+                    cnt = _count(feed_mask(s))
+                    mask = _common(topo, core, dsts, K_RELAY)
+                    g.wait_ge(T.sem.au, cnt)
+                    left = _send(g, T, topo, T.ud, T["ua%d" % j], T.sem["su%d" % j], dsts, mask)
+                    g.wait_ge(T.sem.av, cnt)
+                    left += _send(g, T, topo, T.vd, T["vb%d" % j], T.sem["sv%d" % j], dsts, mask)
                     g.wait_ge(T.sem.sent, left)
         return
 
     mine = T["w%d" % rank]
-    g.sync.dma_start(T.utb[:], T.ut[:]).then_inc(T.sem.ld, 16)
-    g.scalar.dma_start(T.vtb[:], T.vt[:]).then_inc(T.sem.ld, 16)
-    g.sync.dma_start(T.xb[:], T.x[:]).then_inc(T.sem.ldx, 16)
+    g.sync.dma_start(T.ud[:], T.u[:]).then_inc(T.sem.lu, 16)
+    g.scalar.dma_start(T.vd[0:H, :], T.vt[:, 0:H]).then_inc(T.sem.lv, 16)
+    g.sync.dma_start(T.vd[H:128, :], T.vt[:, H:128]).then_inc(T.sem.lv, 16)
+    g.scalar.dma_start(T.utb[:], T.ut[:]).then_inc(T.sem.ld, 16)
+    g.sync.dma_start(T.vtb[:], T.vt[:]).then_inc(T.sem.ld, 16)
+    g.scalar.dma_start(T.xb[:], T.x[:]).then_inc(T.sem.ldx, 16)
 
     g.tensor.wait_ge(T.sem.ld, 32)
     g.tensor.matmul(T.pw[:, 0:128], T.utb[:], T.vtb[:], True, True).then_inc(T.sem.mm, 1)
@@ -103,33 +125,62 @@ def rank_program(g, core, T, topo):
     g.vector.tensor_copy(mine[:], T.pw[:, 0:128]).then_inc(T.sem.wr, 1)
 
     helpers = [h for h, _d in relays[core]]
-    mask = _common(topo, core, helpers + near[core], K_RANK)
-    g.wait_ge(T.sem.wr, 1)
     left = 0
     if helpers:
-        left += _send(g, T, topo, rank, helpers, mask)
+        g.wait_ge(T.sem.lu, 16)
+        left += _send(g, T, topo, T.ud, T.ud, T.sem.au, helpers, feed_mask(core))
+        g.wait_ge(T.sem.lv, 32)
+        left += _send(g, T, topo, T.vd, T.vd, T.sem.av, helpers, feed_mask(core))
+    else:
+        g.wait_ge(T.sem.lu, 16)
+        g.wait_ge(T.sem.lv, 32)
+    g.wait_ge(T.sem.wr, 1)
     if near[core]:
-        left += _send(g, T, topo, rank, near[core], mask)
+        left += _send(g, T, topo, mine, mine, T.sem["arr%d" % rank], near[core], near_mask(core))
+
+    direct = [(j, _count(near_mask(s))) for j, s in enumerate(cores) if core in near[s]]
+    relayed = []
+    for j, s in enumerate(cores):
+        for pos, (h, dsts) in enumerate(relays[s]):
+            if core in dsts:
+                relayed.append((pos + dsts.index(core), j, _count(_common(topo, h, dsts, K_RELAY))))
+    relayed.sort()
+    total = 1 + len(direct) + len(relayed)
+    step = [0]
+
+    def add(lo_l, lo_r, hi_l, hi_r):
+        first, last = step[0] == 0, step[0] == total - 1
+        a = g.tensor.matmul(T.py0[0:H, 0:16], lo_l, lo_r, first, last)
+        b = g.tensor.matmul(T.py1[H:128, 0:16], hi_l, hi_r, first, last)
+        if last:
+            a.then_inc(T.sem.done, 1)
+            b.then_inc(T.sem.done, 1)
+        step[0] += 1
 
     g.tensor.wait_ge(T.sem.wr, 1)
     g.tensor.wait_ge(T.sem.ldx, 16)
-    g.tensor.matmul(T.py[:, 0:16], mine[:], T.xb[:], True, False)
-    order = []
-    for j, s in enumerate(cores):
-        if core in near[s]:
-            order.append((j, _count(_common(topo, s, [h for h, _d in relays[s]] + near[s], K_RANK))))
-    for j, s in enumerate(cores):
-        for h, dsts in relays[s]:
-            if core in dsts:
-                order.append((j, _count(_common(topo, h, dsts, K_RELAY))))
-    for n, (j, cnt) in enumerate(order):
+    add(mine[:, 0:H], T.xb[:], mine[:, H:128], T.xb[:])
+    for j, cnt in direct:
         g.tensor.wait_ge(T.sem["arr%d" % j], cnt)
-        mm = g.tensor.matmul(T.py[:, 0:16], T["w%d" % j][:], T.xb[:], False, n == len(order) - 1)
-    mm.then_inc(T.sem.done, 1)
+        w = T["w%d" % j]
+        add(w[:, 0:H], T.xb[:], w[:, H:128], T.xb[:])
+    for i, (_p, j, cnt) in enumerate(relayed):
+        pt, ua = T["pt%d" % i], T["ua%d" % j]
+        g.tensor.wait_ge(T.sem["su%d" % j], cnt)
+        g.tensor.matmul(pt[0:H, 0:16], ua[:], T.xb[:], True, True).then_inc(T.sem["tm%d" % j], 1)
+        g.tensor.matmul(pt[H:128, 0:16], ua[:], T.xb[:], True, True).then_inc(T.sem["tm%d" % j], 1)
+        g.vector.wait_ge(T.sem["tm%d" % j], 2)
+        g.vector.tensor_copy(T["tb%d" % j][:], pt[:, 0:16]).then_inc(T.sem["tc%d" % j], 1)
+    for _p, j, cnt in relayed:
+        vb, tb = T["vb%d" % j], T["tb%d" % j]
+        g.tensor.wait_ge(T.sem["tc%d" % j], 1)
+        g.tensor.wait_ge(T.sem["sv%d" % j], cnt)
+        add(vb[0:H, :], tb[0:H, :], vb[H:128, :], tb[H:128, :])
 
-    g.vector.wait_ge(T.sem.done, 1)
-    g.vector.tensor_copy(T.ysb[:], T.py[:, 0:16]).then_inc(T.sem.yr, 1)
-    g.sync.wait_ge(T.sem.yr, 1)
+    g.vector.wait_ge(T.sem.done, 2)
+    g.vector.tensor_copy(T.ysb[0:H, :], T.py0[0:H, 0:16]).then_inc(T.sem.yr, 1)
+    g.vector.tensor_copy(T.ysb[H:128, :], T.py1[H:128, 0:16]).then_inc(T.sem.yr, 1)
+    g.sync.wait_ge(T.sem.yr, 2)
     g.sync.dma_start(T.y[:], T.ysb[:]).then_inc(T.sem.st, 16)
     g.sync.wait_ge(T.sem.st, 16)
     g.wait_ge(T.sem.sent, left)

from concourse.bass import DstId, RemoteDMATransfer

N = 7
NCORES = 128
K_FEED = 4
K_NEAR = 8
K_RELAY = 8
H = 64

SCRATCH = {
    "ud": ("dram", [128, 64], "bfloat16"),
    "vd": ("dram", [128, 64], "bfloat16"),
    "utb": ("sbuf", [64, 128], "bfloat16"),
    "vtb": ("sbuf", [64, 128], "bfloat16"),
    "xb": ("sbuf", [128, 16], "bfloat16"),
    "ysb": ("sbuf", [128, 16], "bfloat16"),
    "pw": ("psum", [128, 512], "float32"),
    "py0": ("psum", [128, 512], "float32"),
    "py1": ("psum", [128, 512], "float32"),
}
for _j in range(N):
    SCRATCH["w%d" % _j] = ("sbuf", [128, 128], "bfloat16")
    SCRATCH["ua%d" % _j] = ("sbuf", [128, 64], "bfloat16")
    SCRATCH["vb%d" % _j] = ("sbuf", [128, 64], "bfloat16")
    SCRATCH["tb%d" % _j] = ("sbuf", [128, 16], "bfloat16")
for _i in range(5):
    SCRATCH["pt%d" % _i] = ("psum", [128, 512], "float32")

SEMAPHORES = ["lu", "lv", "ld", "ldx", "mm", "wr", "sent", "done", "yr", "st", "au", "av"]
for _j in range(N):
    SEMAPHORES += ["arr%d" % _j, "su%d" % _j, "sv%d" % _j, "tm%d" % _j, "tc%d" % _j]


def _count(mask):
    return bin(mask).count("1")


def _engines(mask, k):
    out, bit = 0, 1
    while _count(out) < k and bit <= mask:
        out |= mask & bit
        bit <<= 1
    return out


def _common(topo, src, dsts, k):
    m = topo.mask(src, dsts[0])
    for d in dsts[1:]:
        m &= topo.mask(src, d)
    return _engines(m, k)


def _plan(cores, topo):
    near, far, load = {}, {}, {}
    for i, s in enumerate(cores):
        turn = cores[i + 1:] + cores[:i]
        near[s] = [d for d in turn if topo.may_write(s, d)]
        far[s] = [d for d in turn if not topo.may_write(s, d)]
        for d in near[s]:
            key = (d, topo.die(s))
            load[key] = load.get(key, 0) + 1
    relays = {}
    for s in cores:
        ports = [c for c in range(NCORES)
                 if topo.chip(c) == topo.chip(s) and c not in cores and all(topo.may_write(c, d) for d in far[s])]
        chosen = {}
        for c in ports:
            chosen[c] = []
        for d in far[s]:
            best = min(ports, key=lambda c: (len(chosen[c]), load.get((d, topo.die(c)), 0), c))
            chosen[best].append(d)
            key = (d, topo.die(best))
            load[key] = load.get(key, 0) + 1
        relays[s] = sorted([kv for kv in chosen.items() if kv[1]], key=lambda kv: (-len(kv[1]), kv[0]))
    return near, relays


def _send(g, T, topo, src, dst, sem, dsts, mask):
    ids = []
    for d in dsts:
        rid, pid, _se = topo.addr(d)
        ids.append(DstId(rid=rid, pnc=pid))
    g.remote_dma_fused(
        [RemoteDMATransfer(dst_ids=ids, dma_engine_mask=mask, remote_sem=sem,
                           srcs=[src[:]], dsts=[dst[:] for _d in dsts], alu_op=0)],
        local_sem=T.sem.sent)
    return _count(mask)


def rank_program(g, core, T, topo):
    cores = list(T.cores)
    near, relays = _plan(cores, topo)
    rank = T.rank_of(core)

    def feed_mask(s):
        return _common(topo, s, [h for h, _d in relays[s]] + near[s], K_FEED)

    def near_mask(s):
        return _common(topo, s, [h for h, _d in relays[s]] + near[s], K_NEAR)

    if rank is None:
        for j, s in enumerate(cores):
            for h, dsts in relays[s]:
                if h == core:
                    cnt = _count(feed_mask(s))
                    mask = _common(topo, core, dsts, K_RELAY)
                    g.wait_ge(T.sem.au, cnt)
                    left = _send(g, T, topo, T.ud, T["ua%d" % j], T.sem["su%d" % j], dsts, mask)
                    g.wait_ge(T.sem.av, cnt)
                    left += _send(g, T, topo, T.vd, T["vb%d" % j], T.sem["sv%d" % j], dsts, mask)
                    g.wait_ge(T.sem.sent, left)
        return

    mine = T["w%d" % rank]
    g.sync.dma_start(T.ud[:], T.u[:]).then_inc(T.sem.lu, 16)
    g.scalar.dma_start(T.vd[0:H, :], T.vt[:, 0:H]).then_inc(T.sem.lv, 16)
    g.sync.dma_start(T.vd[H:128, :], T.vt[:, H:128]).then_inc(T.sem.lv, 16)
    g.scalar.dma_start(T.utb[:], T.ut[:]).then_inc(T.sem.ld, 16)
    g.sync.dma_start(T.vtb[:], T.vt[:]).then_inc(T.sem.ld, 16)
    g.scalar.dma_start(T.xb[:], T.x[:]).then_inc(T.sem.ldx, 16)

    g.tensor.wait_ge(T.sem.ld, 32)
    g.tensor.matmul(T.pw[:, 0:128], T.utb[:], T.vtb[:], True, True).then_inc(T.sem.mm, 1)
    g.vector.wait_ge(T.sem.mm, 1)
    g.vector.tensor_copy(mine[:], T.pw[:, 0:128]).then_inc(T.sem.wr, 1)

    helpers = [h for h, _d in relays[core]]
    left = 0
    if helpers:
        g.wait_ge(T.sem.lu, 16)
        left += _send(g, T, topo, T.ud, T.ud, T.sem.au, helpers, feed_mask(core))
        g.wait_ge(T.sem.lv, 32)
        left += _send(g, T, topo, T.vd, T.vd, T.sem.av, helpers, feed_mask(core))
    else:
        g.wait_ge(T.sem.lu, 16)
        g.wait_ge(T.sem.lv, 32)
    g.wait_ge(T.sem.wr, 1)
    if near[core]:
        left += _send(g, T, topo, mine, mine, T.sem["arr%d" % rank], near[core], near_mask(core))

    direct = [(j, _count(near_mask(s))) for j, s in enumerate(cores) if core in near[s]]
    relayed = []
    for j, s in enumerate(cores):
        for pos, (h, dsts) in enumerate(relays[s]):
            if core in dsts:
                relayed.append((pos + dsts.index(core), j, _count(_common(topo, h, dsts, K_RELAY))))
    relayed.sort()
    total = 1 + len(direct) + len(relayed)
    step = [0]

    def add(lo_l, lo_r, hi_l, hi_r):
        first, last = step[0] == 0, step[0] == total - 1
        a = g.tensor.matmul(T.py0[0:H, 0:16], lo_l, lo_r, first, last)
        b = g.tensor.matmul(T.py1[H:128, 0:16], hi_l, hi_r, first, last)
        if last:
            a.then_inc(T.sem.done, 1)
            b.then_inc(T.sem.done, 1)
        step[0] += 1

    g.tensor.wait_ge(T.sem.wr, 1)
    g.tensor.wait_ge(T.sem.ldx, 16)
    add(mine[:, 0:H], T.xb[:], mine[:, H:128], T.xb[:])
    for j, cnt in direct:
        g.tensor.wait_ge(T.sem["arr%d" % j], cnt)
        w = T["w%d" % j]
        add(w[:, 0:H], T.xb[:], w[:, H:128], T.xb[:])
    for i, (_p, j, cnt) in enumerate(relayed):
        pt, ua = T["pt%d" % i], T["ua%d" % j]
        g.tensor.wait_ge(T.sem["su%d" % j], cnt)
        g.tensor.matmul(pt[0:H, 0:16], ua[:], T.xb[:], True, True).then_inc(T.sem["tm%d" % j], 1)
        g.tensor.matmul(pt[H:128, 0:16], ua[:], T.xb[:], True, True).then_inc(T.sem["tm%d" % j], 1)
        g.vector.wait_ge(T.sem["tm%d" % j], 2)
        g.vector.tensor_copy(T["tb%d" % j][:], pt[:, 0:16]).then_inc(T.sem["tc%d" % j], 1)
    for _p, j, cnt in relayed:
        vb, tb = T["vb%d" % j], T["tb%d" % j]
        g.tensor.wait_ge(T.sem["tc%d" % j], 1)
        g.tensor.wait_ge(T.sem["sv%d" % j], cnt)
        add(vb[0:H, :], tb[0:H, :], vb[H:128, :], tb[H:128, :])

    g.vector.wait_ge(T.sem.done, 2)
    g.vector.tensor_copy(T.ysb[0:H, :], T.py0[0:H, 0:16]).then_inc(T.sem.yr, 1)
    g.vector.tensor_copy(T.ysb[H:128, :], T.py1[H:128, 0:16]).then_inc(T.sem.yr, 1)
    g.sync.wait_ge(T.sem.yr, 2)
    g.sync.dma_start(T.y[:], T.ysb[:]).then_inc(T.sem.st, 16)
    g.sync.wait_ge(T.sem.st, 16)
    g.wait_ge(T.sem.sent, left)
